import numpy as np
import ml_dtypes


def mxq(x, axis, fmt="e4m3"):
    dtype, down = {"e4m3": (ml_dtypes.float8_e4m3fn, 7), "e5m2": (ml_dtypes.float8_e5m2, 14)}[fmt]
    v = np.moveaxis(np.asarray(x, np.float32).astype(ml_dtypes.bfloat16).astype(np.float64), axis, -1)
    blocks = v.reshape(v.shape[:-1] + (-1, 32))
    amax = np.abs(blocks).max(-1, keepdims=True)
    byte = np.maximum(np.where(amax > 0, np.frexp(amax)[1] - 1 + 127, 0) - down, 1)
    scale = np.exp2(byte - 127.0)
    codes = (blocks / scale).astype(np.float32).astype(dtype).astype(np.float64)
    return np.moveaxis((codes * scale).reshape(v.shape), -1, axis)


WIDE = False


def mx_kscale(k):
    if not WIDE:
        return np.ones(k)
    levels = np.array([10, -10, 5, -5, 0])
    if k % 512:
        return np.exp2(np.random.permutation(np.resize(levels, k // 32))).repeat(32)
    a = np.empty((k // 512, 16))
    for p in range(k // 512):
        a[p, :8] = np.random.permutation(np.resize(levels, 8))
        for g in range(8):
            far = levels[np.abs(levels - a[p, g]) >= 10]
            a[p, g + 8] = far[np.random.randint(len(far))]
    return np.exp2(a.ravel()).repeat(32)


def f64(x):
    return np.asarray(x).astype(np.float64)


def striped(idx):
    return np.tile(idx.reshape(-1, 16).T, (8, 1)).astype(np.uint16)


def unstriped(offs):
    return offs[:16].T.reshape(-1).astype(np.int64)


def pack_weight(w):
    k, n = w.shape
    w = f64(np.asarray(w, np.float32).astype(ml_dtypes.bfloat16)).reshape(k // 32, 32, n)
    amax = np.abs(w).max(1)
    byte = np.clip(np.where(amax > 0, np.frexp(amax)[1] - 1 + 127 - 7, 1), 1, 254)
    scaled = (w * np.exp2(127.0 - byte)[:, None, :]).reshape(k, n).astype(np.float32)
    words = np.ascontiguousarray(scaled.reshape(k // 512, 128, 4, n).transpose(0, 1, 3, 2)).astype(ml_dtypes.float8_e4m3fn).view(np.uint8)
    return words, np.ascontiguousarray(byte.astype(np.uint8).reshape(k // 512, 16, n))


def unpack_weight(words, scales):
    g, p, n, _ = words.shape
    vals = np.ascontiguousarray(words).view(ml_dtypes.float8_e4m3fn).astype(np.float64) * np.repeat(np.exp2(scales.astype(np.float64) - 127.0), 8, axis=1)[..., None]
    return vals.transpose(0, 1, 3, 2).reshape(g * 512, n)


K, T, S, V, N = 512, 4096, 1024, 512, 128


def setup_inputs():
    n = np.random.standard_normal
    s = mx_kscale(K)[:, None]
    packed_xT = pack_weight(n((K, T)) * s)
    packed_w1 = pack_weight(n((K, N)) / np.sqrt(K) / s)
    packed_w2 = pack_weight(n((K, N)) / np.sqrt(K) / s)
    return {
        "x_words": packed_xT[0],
        "x_scales": packed_xT[1],
        "sT": (n((K, V)) * s).astype(np.float32),
        "w1_words": packed_w1[0],
        "w1_scales": packed_w1[1],
        "w2_words": packed_w2[0],
        "w2_scales": packed_w2[1],
        "offs": striped(np.random.permutation(T)[:S]),
        "par": striped(np.random.randint(0, V, S)),
    }


def reference(x_words, x_scales, sT, w1_words, w1_scales, w2_words, w2_scales, offs, par):
    xq = unpack_weight(x_words, x_scales)[:, unstriped(offs)]
    y = unpack_weight(w1_words, w1_scales).T @ xq
    t = unpack_weight(w2_words, w2_scales).T @ mxq(f64(sT), 0, "e4m3")
    return y + t[:, unstriped(par)]

@@ -1,0 +1,125 @@
+from contextlib import ExitStack
+
+import concourse.mybir as mybir
+
+K, T, S, V, N = 512, 4096, 1024, 512, 128
+FLOPS = 2 * K * N * (S + V)
+
+F32 = mybir.dt.float32
+BF16 = mybir.dt.bfloat16
+I32 = mybir.dt.int32
+U32 = mybir.dt.uint32
+U16 = mybir.dt.uint16
+U8 = mybir.dt.uint8
+FP8X4 = mybir.dt.float8_e4m3fn_x4
+ADD = mybir.AluOpType.add
+
+P = 128
+PACK = 4
+LANES = 16
+HALF_S = S // 2
+HALF_V = V // 2
+PIECE = 256
+
+
+def words_i32(words):
+    return words[0].rearrange("p n t -> p (n t)").bitcast(I32)
+
+
+def load_scale_rows(queue, plane, scales):
+    for r in range(4):
+        queue.dma_start(plane[r:P:32, :].bitcast(I32), scales[0, r:16:4, :].bitcast(I32))
+
+
+def tile_picked_fpn_none_p_kernel(
+    tc, x_words, x_scales, sT, w1_words, w1_scales, w2_words, w2_scales, offs, par, out
+):
+    nc = tc.nc
+    with ExitStack() as ctx:
+        sb = ctx.enter_context(tc.tile_pool(name="sb", bufs=1))
+        ps = ctx.enter_context(tc.psum_pool(name="ps", bufs=1))
+
+        offs_sb = sb.tile([P, S // LANES], U16, name="offs_sb")
+        par_sb = sb.tile([P, S // LANES], U16, name="par_sb")
+        s_raw = sb.tile([P, PACK, V], F32, name="s_raw")
+        x_w = sb.tile([P, T], U32, name="x_w", align_bytes=64)
+        x_s = sb.tile([P, T], U8, name="x_s", tag="early", align_bytes=64)
+        y_s = sb.tile([P, S], U8, name="y_s", align_bytes=64)
+        w1_w = sb.tile([P, N], U32, name="w1_w", align_bytes=64)
+        w2_w = sb.tile([P, N], U32, name="w2_w", align_bytes=64)
+        w_s = sb.tile([P, 2 * N], U8, name="w_s", align_bytes=64)
+
+        nc.sync.dma_start(offs_sb[:], offs)
+        nc.scalar.dma_start(s_raw[:], sT.rearrange("(p j) v -> p j v", j=PACK))
+        nc.sync.dma_start(par_sb[:], par)
+        nc.scalar.dma_start(x_w[:].bitcast(I32), words_i32(x_words))
+        nc.vector.memset(x_s[:].bitcast(I32), 0)
+        nc.vector.memset(y_s[:].bitcast(I32), 0)
+        nc.gpsimd.memset(w_s[:].bitcast(I32), 0)
+        nc.sync.dma_start(x_s[0:P:8, :].bitcast(I32), x_scales[0].bitcast(I32))
+        load_scale_rows(nc.gpsimd, w_s[:, N : 2 * N], w2_scales)
+        load_scale_rows(nc.gpsimd, w_s[:, 0:N], w1_scales)
+        nc.sync.dma_start(w2_w[:].bitcast(I32), words_i32(w2_words))
+        nc.sync.dma_start(w1_w[:].bitcast(I32), words_i32(w1_words))
+
+        def entries(lst, start, count):
+            return lst[:, start // LANES : (start + count) // LANES]
+
+        g_s = sb.tile([P, S], U8, name="g_s", align_bytes=64)
+        nc.vector.tensor_copy(g_s[:], x_s[:].indirect(offs_sb[:]))
+        for r in range(4):
+            nc.sync.dma_start(y_s[r:P:32, :].bitcast(I32), g_s[8 * r : P : 32, :].bitcast(I32))
+
+        t_sb = sb.tile([P, V], F32, name="t_sb", tag="late", align_bytes=64)
+        s_bf = [
+            sb.tile([P, HALF_V, PACK], BF16, name="s_bf%d" % h, tag=tag, align_bytes=64)
+            for h, tag in enumerate(("early", "s_bf1"))
+        ]
+        s_w = [sb.tile([P, HALF_V], U32, name="s_w%d" % h, align_bytes=64) for h in range(2)]
+        s_s = [sb.tile([P, HALF_V], U8, name="s_s%d" % h, align_bytes=64) for h in range(2)]
+        t_ps = [ps.tile([P, HALF_V], F32, name="t_ps%d" % h) for h in range(2)]
+
+        for h, copy in enumerate((nc.vector.tensor_copy, nc.scalar.copy)):
+            copy(
+                s_bf[h][:].rearrange("p (c i) t -> p c t i", i=4),
+                s_raw[:, :, h * HALF_V : (h + 1) * HALF_V].rearrange("p t (c i) -> p c t i", i=4),
+            )
+        for h in (1, 0):
+            nc.vector.quantize_mx(
+                out=s_w[h][:].bitcast(FP8X4), scales=s_s[h][:], in_=s_bf[h][:].rearrange("p v t -> p (v t)")
+            )
+            nc.tensor.matmul_mx(
+                out=t_ps[h][:],
+                lhsT=w2_w[:].bitcast(FP8X4),
+                lhsT_scale=w_s[:, N : 2 * N],
+                rhs=s_w[h][:].bitcast(FP8X4),
+                rhs_scale=s_s[h][:],
+                start=True,
+                stop=True,
+            )
+            nc.scalar.copy(t_sb[:, h * HALF_V : (h + 1) * HALF_V], t_ps[h][:])
+
+        t_g = sb.tile([P, S], F32, name="t_g")
+        for j0 in range(0, S, PIECE):
+            nc.vector.tensor_copy(t_g[:, j0 : j0 + PIECE], t_sb[:].indirect(entries(par_sb, j0, PIECE)))
+
+        g_w = sb.tile([P, S], U32, name="g_w", tag="late", align_bytes=64)
+        for j0 in range(0, S, HALF_S):
+            nc.vector.tensor_copy(g_w[:, j0 : j0 + HALF_S], x_w[:].indirect(entries(offs_sb, j0, HALF_S)))
+
+        res = sb.tile([P, S], F32, name="res")
+        pieces = ((0, 512), (512, 256), (768, 256))
+        for n, (j0, width) in enumerate(pieces):
+            y_ps = ps.tile([P, width], F32, name="y_ps%d" % n)
+            nc.tensor.matmul_mx(
+                out=y_ps[:],
+                lhsT=w1_w[:].bitcast(FP8X4),
+                lhsT_scale=w_s[:, 0:N],
+                rhs=g_w[:, j0 : j0 + width].bitcast(FP8X4),
+                rhs_scale=y_s[:, j0 : j0 + width],
+                start=True,
+                stop=True,
+            )
+            nc.vector.tensor_tensor(res[:, j0 : j0 + width], y_ps[:], t_g[:, j0 : j0 + width], ADD)
+            queue = nc.sync if n % 2 == 0 else nc.scalar
+            queue.dma_start(out[:, j0 : j0 + width], res[:, j0 : j0 + width])

@@ -26,9 +26,9 @@ def words_i32(words):
     return words[0].rearrange("p n t -> p (n t)").bitcast(I32)
 
 
-def load_scale_rows(queue, plane, scales):
-    for r in range(4):
-        queue.dma_start(plane[r:P:32, :].bitcast(I32), scales[0, r:16:4, :].bitcast(I32))
+def load_scale_rows(queue, plane, scales, rs=range(4)):
+    for q in rs:
+        queue.dma_start(plane[32 * q : 32 * q + 4, :].bitcast(I32), scales[0, 4 * q : 4 * q + 4, :].bitcast(I32))
 
 
 def tile_picked_fpn_none_p_kernel(
@@ -41,57 +41,54 @@ def tile_picked_fpn_none_p_kernel(
 
         offs_sb = sb.tile([P, S // LANES], U16, name="offs_sb")
         par_sb = sb.tile([P, S // LANES], U16, name="par_sb")
-        s_raw = sb.tile([P, PACK, V], F32, name="s_raw")
+        s_raw = [sb.tile([P, PACK, HALF_V], F32, name="s_raw%d" % h) for h in range(2)]
         x_w = sb.tile([P, T], U32, name="x_w", align_bytes=64)
-        x_s = sb.tile([P, T], U8, name="x_s", tag="early", align_bytes=64)
+        x_s = sb.tile([P, T], U8, name="x_s", align_bytes=64)
         y_s = sb.tile([P, S], U8, name="y_s", align_bytes=64)
         w1_w = sb.tile([P, N], U32, name="w1_w", align_bytes=64)
         w2_w = sb.tile([P, N], U32, name="w2_w", align_bytes=64)
-        w_s = sb.tile([P, 2 * N], U8, name="w_s", align_bytes=64)
+        w1_s = sb.tile([P, N], U8, name="w1_s", align_bytes=64)
+        w2_s = sb.tile([P, N], U8, name="w2_s", align_bytes=64)
+        s_rows = sT.rearrange("(p j) v -> p j v", j=PACK)
 
-        nc.sync.dma_start(offs_sb[:], offs)
-        nc.scalar.dma_start(s_raw[:], sT.rearrange("(p j) v -> p j v", j=PACK))
-        nc.sync.dma_start(par_sb[:], par)
-        nc.scalar.dma_start(x_w[:].bitcast(I32), words_i32(x_words))
+        nc.gpsimd.memset(w2_s[:].bitcast(I32), 0)
+        nc.gpsimd.memset(w1_s[:].bitcast(I32), 0)
         nc.vector.memset(x_s[:].bitcast(I32), 0)
         nc.vector.memset(y_s[:].bitcast(I32), 0)
-        nc.gpsimd.memset(w_s[:].bitcast(I32), 0)
-        nc.sync.dma_start(x_s[0:P:8, :].bitcast(I32), x_scales[0].bitcast(I32))
-        load_scale_rows(nc.gpsimd, w_s[:, N : 2 * N], w2_scales)
-        load_scale_rows(nc.gpsimd, w_s[:, 0:N], w1_scales)
+        nc.sync.dma_start(offs_sb[:], offs)
+        nc.sync.dma_start(par_sb[:], par)
         nc.sync.dma_start(w2_w[:].bitcast(I32), words_i32(w2_words))
+        nc.sync.dma_start(s_raw[0][:], s_rows[:, :, 0:HALF_V])
+        nc.sync.dma_start(s_raw[1][:], s_rows[:, :, HALF_V:V])
+        load_scale_rows(nc.sync, w2_s, w2_scales)
+        nc.sync.dma_start(x_s[0:P:8, :].bitcast(I32), x_scales[0].bitcast(I32))
+        nc.sync.dma_start(x_w[:].bitcast(I32), words_i32(x_words))
         nc.sync.dma_start(w1_w[:].bitcast(I32), words_i32(w1_words))
+        load_scale_rows(nc.gpsimd, w1_s, w1_scales, (0, 1))
+        load_scale_rows(nc.sync, w1_s, w1_scales, (2, 3))
 
         def entries(lst, start, count):
             return lst[:, start // LANES : (start + count) // LANES]
 
-        g_s = sb.tile([P, S], U8, name="g_s", align_bytes=64)
-        nc.vector.tensor_copy(g_s[:], x_s[:].indirect(offs_sb[:]))
-        for r in range(4):
-            nc.sync.dma_start(y_s[r:P:32, :].bitcast(I32), g_s[8 * r : P : 32, :].bitcast(I32))
-
-        t_sb = sb.tile([P, V], F32, name="t_sb", tag="late", align_bytes=64)
-        s_bf = [
-            sb.tile([P, HALF_V, PACK], BF16, name="s_bf%d" % h, tag=tag, align_bytes=64)
-            for h, tag in enumerate(("early", "s_bf1"))
-        ]
+        t_sb = sb.tile([P, V], F32, name="t_sb")
+        s_bf = [sb.tile([P, HALF_V, PACK], BF16, name="s_bf%d" % h, align_bytes=64) for h in range(2)]
         s_w = [sb.tile([P, HALF_V], U32, name="s_w%d" % h, align_bytes=64) for h in range(2)]
         s_s = [sb.tile([P, HALF_V], U8, name="s_s%d" % h, align_bytes=64) for h in range(2)]
         t_ps = [ps.tile([P, HALF_V], F32, name="t_ps%d" % h) for h in range(2)]
 
-        for h, copy in enumerate((nc.vector.tensor_copy, nc.scalar.copy)):
-            copy(
-                s_bf[h][:].rearrange("p (c i) t -> p c t i", i=4),
-                s_raw[:, :, h * HALF_V : (h + 1) * HALF_V].rearrange("p t (c i) -> p c t i", i=4),
-            )
-        for h in (1, 0):
+        for h in range(2):
+            for copy, cols in ((nc.vector.tensor_copy, slice(0, 160)), (nc.scalar.copy, slice(160, HALF_V))):
+                copy(
+                    s_bf[h][:, cols, :].rearrange("p (c i) t -> p c t i", i=4),
+                    s_raw[h][:, :, cols].rearrange("p t (c i) -> p c t i", i=4),
+                )
             nc.vector.quantize_mx(
                 out=s_w[h][:].bitcast(FP8X4), scales=s_s[h][:], in_=s_bf[h][:].rearrange("p v t -> p (v t)")
             )
             nc.tensor.matmul_mx(
                 out=t_ps[h][:],
                 lhsT=w2_w[:].bitcast(FP8X4),
-                lhsT_scale=w_s[:, N : 2 * N],
+                lhsT_scale=w2_s[:],
                 rhs=s_w[h][:].bitcast(FP8X4),
                 rhs_scale=s_s[h][:],
                 start=True,
@@ -99,27 +96,39 @@ def tile_picked_fpn_none_p_kernel(
             )
             nc.scalar.copy(t_sb[:, h * HALF_V : (h + 1) * HALF_V], t_ps[h][:])
 
-        t_g = sb.tile([P, S], F32, name="t_g")
-        for j0 in range(0, S, PIECE):
-            nc.vector.tensor_copy(t_g[:, j0 : j0 + PIECE], t_sb[:].indirect(entries(par_sb, j0, PIECE)))
+        g_s = sb.tile([P, S], U8, name="g_s", tag="s_bf1", align_bytes=64)
+        nc.vector.tensor_copy(g_s[:], x_s[:].indirect(offs_sb[:]))
+        for q in range(4):
+            nc.sync.dma_start(y_s[32 * q : 32 * q + 4, :].bitcast(I32), g_s[32 * q : 32 * q + 32 : 8, :].bitcast(I32))
 
-        g_w = sb.tile([P, S], U32, name="g_w", tag="late", align_bytes=64)
-        for j0 in range(0, S, HALF_S):
-            nc.vector.tensor_copy(g_w[:, j0 : j0 + HALF_S], x_w[:].indirect(entries(offs_sb, j0, HALF_S)))
+        t_early = sb.tile([P, 3, PIECE], F32, name="t_early", tag="x_s", align_bytes=64)
+        t_g = [t_early[:, n, :] for n in range(3)]
+        for n in range(3):
+            nc.vector.tensor_copy(t_g[n], t_sb[:].indirect(entries(par_sb, n * PIECE, PIECE)))
 
-        res = sb.tile([P, S], F32, name="res")
-        pieces = ((0, 512), (512, 256), (768, 256))
-        for n, (j0, width) in enumerate(pieces):
-            y_ps = ps.tile([P, width], F32, name="y_ps%d" % n)
+        g_w = [sb.tile([P, HALF_S], U32, name="g_w%d" % h, align_bytes=64) for h in range(2)]
+        for h in range(2):
+            nc.vector.tensor_copy(g_w[h][:], x_w[:].indirect(entries(offs_sb, h * HALF_S, HALF_S)))
+
+        for n in range(3, 4):
+            t_late = sb.tile([P, PIECE], F32, name="t_late", tag="x_w", align_bytes=64)
+            t_g.append(t_late[:])
+            nc.vector.tensor_copy(t_g[n], t_sb[:].indirect(entries(par_sb, n * PIECE, PIECE)))
+
+        for n in range(S // PIECE):
+            j0 = n * PIECE
+            h, c0 = divmod(j0, HALF_S)
+            y_ps = ps.tile([P, PIECE], F32, name="y_ps%d" % n)
+            res = sb.tile([P, PIECE], F32, name="res%d" % n)
             nc.tensor.matmul_mx(
                 out=y_ps[:],
                 lhsT=w1_w[:].bitcast(FP8X4),
-                lhsT_scale=w_s[:, 0:N],
-                rhs=g_w[:, j0 : j0 + width].bitcast(FP8X4),
-                rhs_scale=y_s[:, j0 : j0 + width],
+                lhsT_scale=w1_s[:],
+                rhs=g_w[h][:, c0 : c0 + PIECE].bitcast(FP8X4),
+                rhs_scale=y_s[:, j0 : j0 + PIECE],
                 start=True,
                 stop=True,
             )
-            nc.vector.tensor_tensor(res[:, j0 : j0 + width], y_ps[:], t_g[:, j0 : j0 + width], ADD)
+            nc.vector.tensor_tensor(res[:], y_ps[:], t_g[n], ADD)
             queue = nc.sync if n % 2 == 0 else nc.scalar
-            queue.dma_start(out[:, j0 : j0 + width], res[:, j0 : j0 + width])
+            queue.dma_start(out[:, j0 : j0 + PIECE], res[:])

@@ -51,17 +51,17 @@ def tile_picked_fpn_none_p_kernel(
         w2_s = sb.tile([P, N], U8, name="w2_s", align_bytes=64)
         s_rows = sT.rearrange("(p j) v -> p j v", j=PACK)
 
-        nc.gpsimd.memset(w2_s[:].bitcast(I32), 0)
-        nc.gpsimd.memset(w1_s[:].bitcast(I32), 0)
         nc.vector.memset(x_s[:].bitcast(I32), 0)
+        nc.vector.memset(w2_s[:].bitcast(I32), 0)
+        nc.vector.memset(w1_s[:].bitcast(I32), 0)
         nc.vector.memset(y_s[:].bitcast(I32), 0)
         nc.sync.dma_start(offs_sb[:], offs)
+        nc.scalar.dma_start(w2_w[:].bitcast(I32), words_i32(w2_words))
         nc.sync.dma_start(par_sb[:], par)
-        nc.sync.dma_start(w2_w[:].bitcast(I32), words_i32(w2_words))
         nc.sync.dma_start(s_raw[0][:], s_rows[:, :, 0:HALF_V])
+        nc.sync.dma_start(x_s[0:P:8, :].bitcast(I32), x_scales[0].bitcast(I32))
         nc.sync.dma_start(s_raw[1][:], s_rows[:, :, HALF_V:V])
         load_scale_rows(nc.sync, w2_s, w2_scales)
-        nc.sync.dma_start(x_s[0:P:8, :].bitcast(I32), x_scales[0].bitcast(I32))
         nc.sync.dma_start(x_w[:].bitcast(I32), words_i32(x_words))
         nc.sync.dma_start(w1_w[:].bitcast(I32), words_i32(w1_words))
         load_scale_rows(nc.gpsimd, w1_s, w1_scales, (0, 1))
@@ -70,6 +70,11 @@ def tile_picked_fpn_none_p_kernel(
         def entries(lst, start, count):
             return lst[:, start // LANES : (start + count) // LANES]
 
+        g_s = sb.tile([P, S], U8, name="g_s", align_bytes=64)
+        nc.vector.tensor_copy(g_s[:], x_s[:].indirect(offs_sb[:]))
+        for q in range(4):
+            nc.sync.dma_start(y_s[32 * q : 32 * q + 4, :].bitcast(I32), g_s[32 * q : 32 * q + 32 : 8, :].bitcast(I32))
+
         t_sb = sb.tile([P, V], F32, name="t_sb")
         s_bf = [sb.tile([P, HALF_V, PACK], BF16, name="s_bf%d" % h, align_bytes=64) for h in range(2)]
         s_w = [sb.tile([P, HALF_V], U32, name="s_w%d" % h, align_bytes=64) for h in range(2)]
@@ -77,11 +82,11 @@ def tile_picked_fpn_none_p_kernel(
         t_ps = [ps.tile([P, HALF_V], F32, name="t_ps%d" % h) for h in range(2)]
 
         for h in range(2):
-            for copy, cols in ((nc.vector.tensor_copy, slice(0, 160)), (nc.scalar.copy, slice(160, HALF_V))):
-                copy(
-                    s_bf[h][:, cols, :].rearrange("p (c i) t -> p c t i", i=4),
-                    s_raw[h][:, :, cols].rearrange("p t (c i) -> p c t i", i=4),
-                )
+            nc.scalar.copy(
+                s_bf[h][:].rearrange("p (c i) t -> p c t i", i=4),
+                s_raw[h][:].rearrange("p t (c i) -> p c t i", i=4),
+            )
+        for h in range(2):
             nc.vector.quantize_mx(
                 out=s_w[h][:].bitcast(FP8X4), scales=s_s[h][:], in_=s_bf[h][:].rearrange("p v t -> p (v t)")
             )
@@ -96,39 +101,34 @@ def tile_picked_fpn_none_p_kernel(
             )
             nc.scalar.copy(t_sb[:, h * HALF_V : (h + 1) * HALF_V], t_ps[h][:])
 
-        g_s = sb.tile([P, S], U8, name="g_s", tag="s_bf1", align_bytes=64)
-        nc.vector.tensor_copy(g_s[:], x_s[:].indirect(offs_sb[:]))
-        for q in range(4):
-            nc.sync.dma_start(y_s[32 * q : 32 * q + 4, :].bitcast(I32), g_s[32 * q : 32 * q + 32 : 8, :].bitcast(I32))
-
-        t_early = sb.tile([P, 3, PIECE], F32, name="t_early", tag="x_s", align_bytes=64)
-        t_g = [t_early[:, n, :] for n in range(3)]
-        for n in range(3):
-            nc.vector.tensor_copy(t_g[n], t_sb[:].indirect(entries(par_sb, n * PIECE, PIECE)))
+        t_early = sb.tile([P, 3 * PIECE], F32, name="t_early")
+        for j0 in range(0, 3 * PIECE, PIECE):
+            nc.vector.tensor_copy(t_early[:, j0 : j0 + PIECE], t_sb[:].indirect(entries(par_sb, j0, PIECE)))
 
         g_w = [sb.tile([P, HALF_S], U32, name="g_w%d" % h, align_bytes=64) for h in range(2)]
         for h in range(2):
             nc.vector.tensor_copy(g_w[h][:], x_w[:].indirect(entries(offs_sb, h * HALF_S, HALF_S)))
 
-        for n in range(3, 4):
-            t_late = sb.tile([P, PIECE], F32, name="t_late", tag="x_w", align_bytes=64)
-            t_g.append(t_late[:])
-            nc.vector.tensor_copy(t_g[n], t_sb[:].indirect(entries(par_sb, n * PIECE, PIECE)))
+        t_late = sb.tile([P, PIECE], F32, name="t_late", tag="x_w", align_bytes=64)
+        nc.vector.tensor_copy(t_late[:], t_sb[:].indirect(entries(par_sb, 3 * PIECE, PIECE)))
 
-        for n in range(S // PIECE):
-            j0 = n * PIECE
+        pieces = (
+            (0, HALF_S, t_early[:, 0:HALF_S], nc.sync),
+            (HALF_S, PIECE, t_early[:, HALF_S : HALF_S + PIECE], nc.scalar),
+            (HALF_S + PIECE, PIECE, t_late[:], nc.sync),
+        )
+        for n, (j0, width, parents, queue) in enumerate(pieces):
             h, c0 = divmod(j0, HALF_S)
-            y_ps = ps.tile([P, PIECE], F32, name="y_ps%d" % n)
-            res = sb.tile([P, PIECE], F32, name="res%d" % n)
+            y_ps = ps.tile([P, width], F32, name="y_ps%d" % n)
+            res = sb.tile([P, width], F32, name="res%d" % n)
             nc.tensor.matmul_mx(
                 out=y_ps[:],
                 lhsT=w1_w[:].bitcast(FP8X4),
                 lhsT_scale=w1_s[:],
-                rhs=g_w[h][:, c0 : c0 + PIECE].bitcast(FP8X4),
-                rhs_scale=y_s[:, j0 : j0 + PIECE],
+                rhs=g_w[h][:, c0 : c0 + width].bitcast(FP8X4),
+                rhs_scale=y_s[:, j0 : j0 + width],
                 start=True,
                 stop=True,
             )
-            nc.vector.tensor_tensor(res[:], y_ps[:], t_g[n], ADD)
-            queue = nc.sync if n % 2 == 0 else nc.scalar
-            queue.dma_start(out[:, j0 : j0 + PIECE], res[:])
+            nc.vector.tensor_tensor(res[:], y_ps[:], parents, ADD)
+            queue.dma_start(out[:, j0 : j0 + width], res[:])

@@ -16,19 +16,33 @@ ADD = mybir.AluOpType.add
 
 P = 128
 PACK = 4
+QUADRANT = 32
+ROWS = 4
+SPREAD = 8
 LANES = 16
+LINE = 4
 HALF_S = S // 2
 HALF_V = V // 2
 PIECE = 256
+VECTOR_COLUMNS = 96
+MX_ALIGN = 64
 
 
-def words_i32(words):
+def words_as_int32(words):
     return words[0].rearrange("p n t -> p (n t)").bitcast(I32)
 
 
-def load_scale_rows(queue, plane, scales, rs=range(4)):
-    for q in rs:
-        queue.dma_start(plane[32 * q : 32 * q + 4, :].bitcast(I32), scales[0, 4 * q : 4 * q + 4, :].bitcast(I32))
+def quadrant_rows(q):
+    return slice(QUADRANT * q, QUADRANT * q + ROWS)
+
+
+def load_scale_rows(queue, plane, scales, quadrants):
+    for q in quadrants:
+        queue.dma_start(plane[quadrant_rows(q), :].bitcast(I32), scales[0, ROWS * q : ROWS * (q + 1), :].bitcast(I32))
+
+
+def entries(lst, start, count):
+    return lst[:, start // LANES : (start + count) // LANES]
 
 
 def tile_picked_fpn_none_p_kernel(
@@ -42,49 +56,56 @@ def tile_picked_fpn_none_p_kernel(
         offs_sb = sb.tile([P, S // LANES], U16, name="offs_sb")
         par_sb = sb.tile([P, S // LANES], U16, name="par_sb")
         s_raw = [sb.tile([P, PACK, HALF_V], F32, name="s_raw%d" % h) for h in range(2)]
-        x_w = sb.tile([P, T], U32, name="x_w", align_bytes=64)
-        x_s = sb.tile([P, T], U8, name="x_s", align_bytes=64)
-        y_s = sb.tile([P, S], U8, name="y_s", align_bytes=64)
-        w1_w = sb.tile([P, N], U32, name="w1_w", align_bytes=64)
-        w2_w = sb.tile([P, N], U32, name="w2_w", align_bytes=64)
-        w1_s = sb.tile([P, N], U8, name="w1_s", align_bytes=64)
-        w2_s = sb.tile([P, N], U8, name="w2_s", align_bytes=64)
-        s_rows = sT.rearrange("(p j) v -> p j v", j=PACK)
+        x_w = sb.tile([P, T], U32, name="x_w", align_bytes=MX_ALIGN)
+        x_s = sb.tile([P, T], U8, name="x_s", align_bytes=MX_ALIGN)
+        y_s = sb.tile([P, S], U8, name="y_s", align_bytes=MX_ALIGN)
+        w1_w = sb.tile([P, N], U32, name="w1_w", align_bytes=MX_ALIGN)
+        w2_w = sb.tile([P, N], U32, name="w2_w", align_bytes=MX_ALIGN)
+        w1_s = sb.tile([P, N], U8, name="w1_s", align_bytes=MX_ALIGN)
+        w2_s = sb.tile([P, N], U8, name="w2_s", align_bytes=MX_ALIGN)
 
-        nc.vector.memset(x_s[:].bitcast(I32), 0)
-        nc.vector.memset(w2_s[:].bitcast(I32), 0)
-        nc.vector.memset(w1_s[:].bitcast(I32), 0)
-        nc.vector.memset(y_s[:].bitcast(I32), 0)
+        for plane in (x_s, w2_s, w1_s, y_s):
+            nc.vector.memset(plane[:].bitcast(I32), 0)
+
+        s_rows = sT.rearrange("(p j) v -> p j v", j=PACK)
         nc.sync.dma_start(offs_sb[:], offs)
-        nc.scalar.dma_start(w2_w[:].bitcast(I32), words_i32(w2_words))
+        nc.scalar.dma_start(w2_w[:].bitcast(I32), words_as_int32(w2_words))
         nc.sync.dma_start(par_sb[:], par)
         nc.sync.dma_start(s_raw[0][:], s_rows[:, :, 0:HALF_V])
-        nc.sync.dma_start(x_s[0:P:8, :].bitcast(I32), x_scales[0].bitcast(I32))
+        nc.sync.dma_start(x_s[0:P:SPREAD, :].bitcast(I32), x_scales[0].bitcast(I32))
         nc.sync.dma_start(s_raw[1][:], s_rows[:, :, HALF_V:V])
-        load_scale_rows(nc.sync, w2_s, w2_scales)
-        nc.sync.dma_start(x_w[:].bitcast(I32), words_i32(x_words))
-        nc.sync.dma_start(w1_w[:].bitcast(I32), words_i32(w1_words))
+        load_scale_rows(nc.sync, w2_s, w2_scales, range(4))
+        nc.sync.dma_start(x_w[:].bitcast(I32), words_as_int32(x_words))
+        nc.sync.dma_start(w1_w[:].bitcast(I32), words_as_int32(w1_words))
         load_scale_rows(nc.gpsimd, w1_s, w1_scales, (0, 1))
         load_scale_rows(nc.sync, w1_s, w1_scales, (2, 3))
 
-        def entries(lst, start, count):
-            return lst[:, start // LANES : (start + count) // LANES]
+        def gather_scales(h, tag):
+            g_s = sb.tile([P, HALF_S], U8, name="g_s%d" % h, tag=tag, align_bytes=MX_ALIGN)
+            nc.vector.tensor_copy(g_s[:], x_s[:].indirect(entries(offs_sb, h * HALF_S, HALF_S)))
+            for q in range(4):
+                nc.sync.dma_start(
+                    y_s[quadrant_rows(q), h * HALF_S : (h + 1) * HALF_S].bitcast(I32),
+                    g_s[QUADRANT * q : QUADRANT * (q + 1) : SPREAD, :].bitcast(I32),
+                )
 
-        g_s = sb.tile([P, S], U8, name="g_s", align_bytes=64)
-        nc.vector.tensor_copy(g_s[:], x_s[:].indirect(offs_sb[:]))
-        for q in range(4):
-            nc.sync.dma_start(y_s[32 * q : 32 * q + 4, :].bitcast(I32), g_s[32 * q : 32 * q + 32 : 8, :].bitcast(I32))
+        gather_scales(0, "g_s0")
 
         t_sb = sb.tile([P, V], F32, name="t_sb")
-        s_bf = [sb.tile([P, HALF_V, PACK], BF16, name="s_bf%d" % h, align_bytes=64) for h in range(2)]
-        s_w = [sb.tile([P, HALF_V], U32, name="s_w%d" % h, align_bytes=64) for h in range(2)]
-        s_s = [sb.tile([P, HALF_V], U8, name="s_s%d" % h, align_bytes=64) for h in range(2)]
+        s_bf = [sb.tile([P, HALF_V, PACK], BF16, name="s_bf%d" % h, align_bytes=MX_ALIGN) for h in range(2)]
+        s_w = [sb.tile([P, HALF_V], U32, name="s_w%d" % h, align_bytes=MX_ALIGN) for h in range(2)]
+        s_s = [sb.tile([P, HALF_V], U8, name="s_s%d" % h, align_bytes=MX_ALIGN) for h in range(2)]
         t_ps = [ps.tile([P, HALF_V], F32, name="t_ps%d" % h) for h in range(2)]
 
-        for h in range(2):
-            nc.scalar.copy(
-                s_bf[h][:].rearrange("p (c i) t -> p c t i", i=4),
-                s_raw[h][:].rearrange("p t (c i) -> p c t i", i=4),
+        split = HALF_V - VECTOR_COLUMNS
+        for copy, h, cols in (
+            (nc.scalar.copy, 0, slice(0, HALF_V)),
+            (nc.scalar.copy, 1, slice(0, split)),
+            (nc.vector.tensor_copy, 1, slice(split, HALF_V)),
+        ):
+            copy(
+                s_bf[h][:, cols, :].rearrange("p (c i) t -> p c t i", i=LINE),
+                s_raw[h][:, :, cols].rearrange("p t (c i) -> p c t i", i=LINE),
             )
         for h in range(2):
             nc.vector.quantize_mx(
@@ -101,21 +122,24 @@ def tile_picked_fpn_none_p_kernel(
             )
             nc.scalar.copy(t_sb[:, h * HALF_V : (h + 1) * HALF_V], t_ps[h][:])
 
-        t_early = sb.tile([P, 3 * PIECE], F32, name="t_early")
-        for j0 in range(0, 3 * PIECE, PIECE):
+        gather_scales(1, "s_bf1")
+
+        early = S - PIECE
+        t_early = sb.tile([P, early], F32, name="t_early")
+        for j0 in range(0, early, PIECE):
             nc.vector.tensor_copy(t_early[:, j0 : j0 + PIECE], t_sb[:].indirect(entries(par_sb, j0, PIECE)))
 
-        g_w = [sb.tile([P, HALF_S], U32, name="g_w%d" % h, align_bytes=64) for h in range(2)]
+        g_w = [sb.tile([P, HALF_S], U32, name="g_w%d" % h, align_bytes=MX_ALIGN) for h in range(2)]
         for h in range(2):
             nc.vector.tensor_copy(g_w[h][:], x_w[:].indirect(entries(offs_sb, h * HALF_S, HALF_S)))
 
-        t_late = sb.tile([P, PIECE], F32, name="t_late", tag="x_w", align_bytes=64)
-        nc.vector.tensor_copy(t_late[:], t_sb[:].indirect(entries(par_sb, 3 * PIECE, PIECE)))
+        t_late = sb.tile([P, PIECE], F32, name="t_late", tag="g_w0", align_bytes=MX_ALIGN)
+        nc.vector.tensor_copy(t_late[:], t_sb[:].indirect(entries(par_sb, early, PIECE)))
 
         pieces = (
             (0, HALF_S, t_early[:, 0:HALF_S], nc.sync),
-            (HALF_S, PIECE, t_early[:, HALF_S : HALF_S + PIECE], nc.scalar),
-            (HALF_S + PIECE, PIECE, t_late[:], nc.sync),
+            (HALF_S, PIECE, t_early[:, HALF_S:early], nc.scalar),
+            (early, PIECE, t_late[:], nc.sync),
         )
         for n, (j0, width, parents, queue) in enumerate(pieces):
             h, c0 = divmod(j0, HALF_S)

@@ -18,13 +18,14 @@ P = 128
 PACK = 4
 QUADRANT = 32
 ROWS = 4
-SPREAD = 8
+X_ROWS = P - 16
 LANES = 16
 LINE = 4
 HALF_S = S // 2
 HALF_V = V // 2
 PIECE = 256
-VECTOR_COLUMNS = 96
+SPARE = 32
+VECTOR_COLUMNS = 128
 MX_ALIGN = 64
 
 
@@ -64,34 +65,34 @@ def tile_picked_fpn_none_p_kernel(
         w1_s = sb.tile([P, N], U8, name="w1_s", align_bytes=MX_ALIGN)
         w2_s = sb.tile([P, N], U8, name="w2_s", align_bytes=MX_ALIGN)
 
-        for plane in (x_s, w2_s, w1_s, y_s):
-            nc.vector.memset(plane[:].bitcast(I32), 0)
+        nc.vector.memset(w2_s[:].bitcast(I32), 0)
+        nc.vector.memset(w1_s[:].bitcast(I32), 0)
+        nc.vector.memset(x_s[0:X_ROWS, :].bitcast(I32), 0)
+        nc.vector.memset(y_s[:].bitcast(I32), 0)
 
         s_rows = sT.rearrange("(p j) v -> p j v", j=PACK)
         nc.sync.dma_start(offs_sb[:], offs)
-        nc.scalar.dma_start(w2_w[:].bitcast(I32), words_as_int32(w2_words))
+        nc.scalar.dma_start(x_s[X_ROWS:P, :].bitcast(I32), x_scales[0].bitcast(I32))
         nc.sync.dma_start(par_sb[:], par)
         nc.sync.dma_start(s_raw[0][:], s_rows[:, :, 0:HALF_V])
-        nc.sync.dma_start(x_s[0:P:SPREAD, :].bitcast(I32), x_scales[0].bitcast(I32))
         nc.sync.dma_start(s_raw[1][:], s_rows[:, :, HALF_V:V])
+        nc.sync.dma_start(w2_w[:].bitcast(I32), words_as_int32(w2_words))
         load_scale_rows(nc.sync, w2_s, w2_scales, range(4))
         nc.sync.dma_start(x_w[:].bitcast(I32), words_as_int32(x_words))
         nc.sync.dma_start(w1_w[:].bitcast(I32), words_as_int32(w1_words))
         load_scale_rows(nc.gpsimd, w1_s, w1_scales, (0, 1))
         load_scale_rows(nc.sync, w1_s, w1_scales, (2, 3))
 
-        def gather_scales(h, tag):
-            g_s = sb.tile([P, HALF_S], U8, name="g_s%d" % h, tag=tag, align_bytes=MX_ALIGN)
-            nc.vector.tensor_copy(g_s[:], x_s[:].indirect(entries(offs_sb, h * HALF_S, HALF_S)))
-            for q in range(4):
-                nc.sync.dma_start(
-                    y_s[quadrant_rows(q), h * HALF_S : (h + 1) * HALF_S].bitcast(I32),
-                    g_s[QUADRANT * q : QUADRANT * (q + 1) : SPREAD, :].bitcast(I32),
-                )
+        g_s = sb.tile([P, S], U8, name="g_s", align_bytes=MX_ALIGN)
+        nc.vector.tensor_copy(g_s[:], x_s[:].indirect(offs_sb[:]))
+        for q in range(4):
+            nc.sync.dma_start(
+                y_s[quadrant_rows(q), :].bitcast(I32),
+                g_s[X_ROWS + ROWS * q : X_ROWS + ROWS * (q + 1), :].bitcast(I32),
+            )
 
-        gather_scales(0, "g_s0")
-
-        t_sb = sb.tile([P, V], F32, name="t_sb")
+        t_sb = sb.tile([P, V + SPARE], F32, name="t_sb")
+        nc.vector.memset(t_sb[:, V:], 0.0)
         s_bf = [sb.tile([P, HALF_V, PACK], BF16, name="s_bf%d" % h, align_bytes=MX_ALIGN) for h in range(2)]
         s_w = [sb.tile([P, HALF_V], U32, name="s_w%d" % h, align_bytes=MX_ALIGN) for h in range(2)]
         s_s = [sb.tile([P, HALF_V], U8, name="s_s%d" % h, align_bytes=MX_ALIGN) for h in range(2)]
@@ -122,26 +123,16 @@ def tile_picked_fpn_none_p_kernel(
             )
             nc.scalar.copy(t_sb[:, h * HALF_V : (h + 1) * HALF_V], t_ps[h][:])
 
-        gather_scales(1, "s_bf1")
-
-        early = S - PIECE
-        t_early = sb.tile([P, early], F32, name="t_early")
-        for j0 in range(0, early, PIECE):
-            nc.vector.tensor_copy(t_early[:, j0 : j0 + PIECE], t_sb[:].indirect(entries(par_sb, j0, PIECE)))
+        t_g = sb.tile([P, S], F32, name="t_g")
+        for j0 in range(0, S, HALF_S):
+            nc.vector.tensor_copy(t_g[:, j0 : j0 + HALF_S], t_sb[:].indirect(entries(par_sb, j0, HALF_S)))
 
         g_w = [sb.tile([P, HALF_S], U32, name="g_w%d" % h, align_bytes=MX_ALIGN) for h in range(2)]
         for h in range(2):
             nc.vector.tensor_copy(g_w[h][:], x_w[:].indirect(entries(offs_sb, h * HALF_S, HALF_S)))
 
-        t_late = sb.tile([P, PIECE], F32, name="t_late", tag="g_w0", align_bytes=MX_ALIGN)
-        nc.vector.tensor_copy(t_late[:], t_sb[:].indirect(entries(par_sb, early, PIECE)))
-
-        pieces = (
-            (0, HALF_S, t_early[:, 0:HALF_S], nc.sync),
-            (HALF_S, PIECE, t_early[:, HALF_S:early], nc.scalar),
-            (early, PIECE, t_late[:], nc.sync),
-        )
-        for n, (j0, width, parents, queue) in enumerate(pieces):
+        pieces = ((0, HALF_S, nc.sync), (HALF_S, PIECE, nc.scalar), (S - PIECE, PIECE, nc.sync))
+        for n, (j0, width, queue) in enumerate(pieces):
             h, c0 = divmod(j0, HALF_S)
             y_ps = ps.tile([P, width], F32, name="y_ps%d" % n)
             res = sb.tile([P, width], F32, name="res%d" % n)
@@ -154,5 +145,5 @@ def tile_picked_fpn_none_p_kernel(
                 start=True,
                 stop=True,
             )
-            nc.vector.tensor_tensor(res[:], y_ps[:], parents, ADD)
+            nc.vector.tensor_tensor(res[:], y_ps[:], t_g[:, j0 : j0 + width], ADD)
             queue.dma_start(out[:, j0 : j0 + width], res[:])

@@ -25,7 +25,7 @@ HALF_S = S // 2
 HALF_V = V // 2
 PIECE = 256
 SPARE = 32
-VECTOR_COLUMNS = 128
+VECTOR_COLUMNS = 64
 MX_ALIGN = 64
 
 
@@ -94,34 +94,38 @@ def tile_picked_fpn_none_p_kernel(
         t_sb = sb.tile([P, V + SPARE], F32, name="t_sb")
         nc.vector.memset(t_sb[:, V:], 0.0)
         s_bf = [sb.tile([P, HALF_V, PACK], BF16, name="s_bf%d" % h, align_bytes=MX_ALIGN) for h in range(2)]
-        s_w = [sb.tile([P, HALF_V], U32, name="s_w%d" % h, align_bytes=MX_ALIGN) for h in range(2)]
-        s_s = [sb.tile([P, HALF_V], U8, name="s_s%d" % h, align_bytes=MX_ALIGN) for h in range(2)]
-        t_ps = [ps.tile([P, HALF_V], F32, name="t_ps%d" % h) for h in range(2)]
 
         split = HALF_V - VECTOR_COLUMNS
         for copy, h, cols in (
             (nc.scalar.copy, 0, slice(0, HALF_V)),
-            (nc.scalar.copy, 1, slice(0, split)),
+            (nc.scalar.copy, 1, slice(0, HALF_V // 2)),
             (nc.vector.tensor_copy, 1, slice(split, HALF_V)),
+            (nc.scalar.copy, 1, slice(HALF_V // 2, split)),
         ):
             copy(
                 s_bf[h][:, cols, :].rearrange("p (c i) t -> p c t i", i=LINE),
                 s_raw[h][:, :, cols].rearrange("p t (c i) -> p c t i", i=LINE),
             )
-        for h in range(2):
+        for n, (h, c0, width) in enumerate(((0, 0, HALF_V), (1, 0, HALF_V // 2), (1, HALF_V // 2, HALF_V // 2))):
+            s_w = sb.tile([P, width], U32, name="s_w%d" % n, align_bytes=MX_ALIGN)
+            s_s = sb.tile([P, width], U8, name="s_s%d" % n, align_bytes=MX_ALIGN)
+            t_ps = ps.tile([P, width], F32, name="t_ps%d" % n)
             nc.vector.quantize_mx(
-                out=s_w[h][:].bitcast(FP8X4), scales=s_s[h][:], in_=s_bf[h][:].rearrange("p v t -> p (v t)")
+                out=s_w[:].bitcast(FP8X4),
+                scales=s_s[:],
+                in_=s_bf[h][:, c0 : c0 + width, :].rearrange("p v t -> p (v t)"),
             )
             nc.tensor.matmul_mx(
-                out=t_ps[h][:],
+                out=t_ps[:],
                 lhsT=w2_w[:].bitcast(FP8X4),
                 lhsT_scale=w2_s[:],
-                rhs=s_w[h][:].bitcast(FP8X4),
-                rhs_scale=s_s[h][:],
+                rhs=s_w[:].bitcast(FP8X4),
+                rhs_scale=s_s[:],
                 start=True,
                 stop=True,
             )
-            nc.scalar.copy(t_sb[:, h * HALF_V : (h + 1) * HALF_V], t_ps[h][:])
+            v0 = h * HALF_V + c0
+            nc.scalar.copy(t_sb[:, v0 : v0 + width], t_ps[:])
 
         t_g = sb.tile([P, S], F32, name="t_g")
         for j0 in range(0, S, HALF_S):
@@ -131,7 +135,13 @@ def tile_picked_fpn_none_p_kernel(
         for h in range(2):
             nc.vector.tensor_copy(g_w[h][:], x_w[:].indirect(entries(offs_sb, h * HALF_S, HALF_S)))
 
-        pieces = ((0, HALF_S, nc.sync), (HALF_S, PIECE, nc.scalar), (S - PIECE, PIECE, nc.sync))
+        pieces = (
+            (0, PIECE, nc.sync),
+            (PIECE, PIECE, nc.scalar),
+            (HALF_S, PIECE, nc.sync),
+            (HALF_S + PIECE, PIECE // 2, nc.scalar),
+            (S - PIECE // 2, PIECE // 2, nc.sync),
+        )
         for n, (j0, width, queue) in enumerate(pieces):
             h, c0 = divmod(j0, HALF_S)
             y_ps = ps.tile([P, width], F32, name="y_ps%d" % n)

@@ -25,7 +25,9 @@ HALF_S = S // 2
 HALF_V = V // 2
 PIECE = 256
 SPARE = 32
-VECTOR_COLUMNS = 64
+GROUP = 128
+SPLIT = 320
+PAIR = 2
 MX_ALIGN = 64
 
 
@@ -56,7 +58,7 @@ def tile_picked_fpn_none_p_kernel(
 
         offs_sb = sb.tile([P, S // LANES], U16, name="offs_sb")
         par_sb = sb.tile([P, S // LANES], U16, name="par_sb")
-        s_raw = [sb.tile([P, PACK, HALF_V], F32, name="s_raw%d" % h) for h in range(2)]
+        s_raw = sb.tile([P, PACK, V], F32, name="s_raw")
         x_w = sb.tile([P, T], U32, name="x_w", align_bytes=MX_ALIGN)
         x_s = sb.tile([P, T], U8, name="x_s", align_bytes=MX_ALIGN)
         y_s = sb.tile([P, S], U8, name="y_s", align_bytes=MX_ALIGN)
@@ -74,8 +76,8 @@ def tile_picked_fpn_none_p_kernel(
         nc.sync.dma_start(offs_sb[:], offs)
         nc.scalar.dma_start(x_s[X_ROWS:P, :].bitcast(I32), x_scales[0].bitcast(I32))
         nc.sync.dma_start(par_sb[:], par)
-        nc.sync.dma_start(s_raw[0][:], s_rows[:, :, 0:HALF_V])
-        nc.sync.dma_start(s_raw[1][:], s_rows[:, :, HALF_V:V])
+        nc.sync.dma_start(s_raw[:, 0:PAIR, :], s_rows[:, 0:PAIR, :])
+        nc.sync.dma_start(s_raw[:, PAIR:PACK, :], s_rows[:, PAIR:PACK, :])
         nc.sync.dma_start(w2_w[:].bitcast(I32), words_as_int32(w2_words))
         load_scale_rows(nc.sync, w2_s, w2_scales, range(4))
         nc.sync.dma_start(x_w[:].bitcast(I32), words_as_int32(x_words))
@@ -93,27 +95,29 @@ def tile_picked_fpn_none_p_kernel(
 
         t_sb = sb.tile([P, V + SPARE], F32, name="t_sb")
         nc.vector.memset(t_sb[:, V:], 0.0)
-        s_bf = [sb.tile([P, HALF_V, PACK], BF16, name="s_bf%d" % h, align_bytes=MX_ALIGN) for h in range(2)]
+        s_bf = sb.tile([P, V, PACK], BF16, name="s_bf", align_bytes=MX_ALIGN)
 
-        split = HALF_V - VECTOR_COLUMNS
-        for copy, h, cols in (
-            (nc.scalar.copy, 0, slice(0, HALF_V)),
-            (nc.scalar.copy, 1, slice(0, HALF_V // 2)),
-            (nc.vector.tensor_copy, 1, slice(split, HALF_V)),
-            (nc.scalar.copy, 1, slice(HALF_V // 2, split)),
+        for rows, c0, c1 in (
+            (slice(0, PAIR), 0, SPLIT),
+            (slice(PAIR, PACK), 0, GROUP),
+            (slice(PAIR, PACK), GROUP, 2 * GROUP),
+            (slice(PAIR, PACK), 2 * GROUP, SPLIT),
         ):
-            copy(
-                s_bf[h][:, cols, :].rearrange("p (c i) t -> p c t i", i=LINE),
-                s_raw[h][:, :, cols].rearrange("p t (c i) -> p c t i", i=LINE),
+            nc.scalar.copy(s_bf[:, c0:c1, rows], s_raw[:, rows, c0:c1].rearrange("p t c -> p c t"))
+        for c0, c1 in ((V - GROUP, V), (SPLIT, V - GROUP)):
+            nc.vector.tensor_copy(
+                s_bf[:, c0:c1, :].rearrange("p (c i) t -> p c t i", i=LINE),
+                s_raw[:, :, c0:c1].rearrange("p t (c i) -> p c t i", i=LINE),
             )
-        for n, (h, c0, width) in enumerate(((0, 0, HALF_V), (1, 0, HALF_V // 2), (1, HALF_V // 2, HALF_V // 2))):
+        width = GROUP
+        for n, v0 in enumerate((V - GROUP, 0, GROUP, 2 * GROUP)):
             s_w = sb.tile([P, width], U32, name="s_w%d" % n, align_bytes=MX_ALIGN)
             s_s = sb.tile([P, width], U8, name="s_s%d" % n, align_bytes=MX_ALIGN)
             t_ps = ps.tile([P, width], F32, name="t_ps%d" % n)
             nc.vector.quantize_mx(
                 out=s_w[:].bitcast(FP8X4),
                 scales=s_s[:],
-                in_=s_bf[h][:, c0 : c0 + width, :].rearrange("p v t -> p (v t)"),
+                in_=s_bf[:, v0 : v0 + width, :].rearrange("p v t -> p (v t)"),
             )
             nc.tensor.matmul_mx(
                 out=t_ps[:],
@@ -124,7 +128,6 @@ def tile_picked_fpn_none_p_kernel(
                 start=True,
                 stop=True,
             )
-            v0 = h * HALF_V + c0
             nc.scalar.copy(t_sb[:, v0 : v0 + width], t_ps[:])
 
         t_g = sb.tile([P, S], F32, name="t_g")
@@ -135,17 +138,14 @@ def tile_picked_fpn_none_p_kernel(
         for h in range(2):
             nc.vector.tensor_copy(g_w[h][:], x_w[:].indirect(entries(offs_sb, h * HALF_S, HALF_S)))
 
-        pieces = (
-            (0, PIECE, nc.sync),
-            (PIECE, PIECE, nc.scalar),
-            (HALF_S, PIECE, nc.sync),
-            (HALF_S + PIECE, PIECE // 2, nc.scalar),
-            (S - PIECE // 2, PIECE // 2, nc.sync),
+        products = (
+            (0, HALF_S, ((PIECE, nc.sync), (PIECE, nc.scalar))),
+            (HALF_S, PIECE, ((PIECE, nc.sync),)),
+            (HALF_S + PIECE, PIECE, ((PIECE // 2, nc.scalar), (PIECE // 2, nc.sync))),
         )
-        for n, (j0, width, queue) in enumerate(pieces):
+        for n, (j0, width, pieces) in enumerate(products):
             h, c0 = divmod(j0, HALF_S)
             y_ps = ps.tile([P, width], F32, name="y_ps%d" % n)
-            res = sb.tile([P, width], F32, name="res%d" % n)
             nc.tensor.matmul_mx(
                 out=y_ps[:],
                 lhsT=w1_w[:].bitcast(FP8X4),
@@ -155,5 +155,10 @@ def tile_picked_fpn_none_p_kernel(
                 start=True,
                 stop=True,
             )
-            nc.vector.tensor_tensor(res[:], y_ps[:], t_g[:, j0 : j0 + width], ADD)
-            queue.dma_start(out[:, j0 : j0 + width], res[:])
+            done = 0
+            for piece, queue in pieces:
+                cols = slice(j0 + done, j0 + done + piece)
+                res = sb.tile([P, piece], F32, name="res%d" % (j0 + done))
+                nc.vector.tensor_tensor(res[:], y_ps[:, done : done + piece], t_g[:, cols], ADD)
+                queue.dma_start(out[:, cols], res[:])
+                done = done + piece

@@ -24,7 +24,7 @@ LINE = 4
 HALF_S = S // 2
 HALF_V = V // 2
 PIECE = 256
-SPARE = 32
+SPARE = 865
 GROUP = 128
 SPLIT = 320
 PAIR = 2
@@ -67,10 +67,7 @@ def tile_picked_fpn_none_p_kernel(
         w1_s = sb.tile([P, N], U8, name="w1_s", align_bytes=MX_ALIGN)
         w2_s = sb.tile([P, N], U8, name="w2_s", align_bytes=MX_ALIGN)
 
-        nc.vector.memset(w2_s[:].bitcast(I32), 0)
-        nc.vector.memset(w1_s[:].bitcast(I32), 0)
         nc.vector.memset(x_s[0:X_ROWS, :].bitcast(I32), 0)
-        nc.vector.memset(y_s[:].bitcast(I32), 0)
 
         s_rows = sT.rearrange("(p j) v -> p j v", j=PACK)
         nc.sync.dma_start(offs_sb[:], offs)
@@ -131,34 +128,33 @@ def tile_picked_fpn_none_p_kernel(
             nc.scalar.copy(t_sb[:, v0 : v0 + width], t_ps[:])
 
         t_g = sb.tile([P, S], F32, name="t_g")
-        for j0 in range(0, S, HALF_S):
-            nc.vector.tensor_copy(t_g[:, j0 : j0 + HALF_S], t_sb[:].indirect(entries(par_sb, j0, HALF_S)))
+        nc.vector.tensor_copy(t_g[:], t_sb[:].indirect(par_sb[:]))
 
         g_w = [sb.tile([P, HALF_S], U32, name="g_w%d" % h, align_bytes=MX_ALIGN) for h in range(2)]
         for h in range(2):
             nc.vector.tensor_copy(g_w[h][:], x_w[:].indirect(entries(offs_sb, h * HALF_S, HALF_S)))
 
-        products = (
-            (0, HALF_S, ((PIECE, nc.sync), (PIECE, nc.scalar))),
-            (HALF_S, PIECE, ((PIECE, nc.sync),)),
-            (HALF_S + PIECE, PIECE, ((PIECE // 2, nc.scalar), (PIECE // 2, nc.sync))),
+        stores = (
+            (0, PIECE, 1, nc.sync),
+            (PIECE, PIECE, 1, nc.scalar),
+            (HALF_S, GROUP, 2, nc.sync),
+            (HALF_S + PIECE, GROUP, 1, nc.scalar),
+            (S - GROUP, GROUP, 1, nc.sync),
         )
-        for n, (j0, width, pieces) in enumerate(products):
-            h, c0 = divmod(j0, HALF_S)
-            y_ps = ps.tile([P, width], F32, name="y_ps%d" % n)
-            nc.tensor.matmul_mx(
-                out=y_ps[:],
-                lhsT=w1_w[:].bitcast(FP8X4),
-                lhsT_scale=w1_s[:],
-                rhs=g_w[h][:, c0 : c0 + width].bitcast(FP8X4),
-                rhs_scale=y_s[:, j0 : j0 + width],
-                start=True,
-                stop=True,
-            )
-            done = 0
-            for piece, queue in pieces:
-                cols = slice(j0 + done, j0 + done + piece)
-                res = sb.tile([P, piece], F32, name="res%d" % (j0 + done))
-                nc.vector.tensor_tensor(res[:], y_ps[:, done : done + piece], t_g[:, cols], ADD)
-                queue.dma_start(out[:, cols], res[:])
-                done = done + piece
+        banks = ["y_ps0", "y_ps1", "y_ps2", "y_ps3", "t_ps0", "t_ps1"]
+        for first, width, count, queue in stores:
+            res = sb.tile([P, width * count], F32, name="res%d" % first)
+            for j0 in range(first, first + width * count, width):
+                h, c0 = divmod(j0, HALF_S)
+                y_ps = ps.tile([P, width], F32, name="y_ps", tag=banks.pop(0))
+                nc.tensor.matmul_mx(
+                    out=y_ps[:],
+                    lhsT=w1_w[:].bitcast(FP8X4),
+                    lhsT_scale=w1_s[:],
+                    rhs=g_w[h][:, c0 : c0 + width].bitcast(FP8X4),
+                    rhs_scale=y_s[:, j0 : j0 + width],
+                    start=True,
+                    stop=True,
+                )
+                nc.vector.tensor_tensor(res[:, j0 - first : j0 - first + width], y_ps[:], t_g[:, j0 : j0 + width], ADD)
+            queue.dma_start(out[:, first : first + width * count], res[:])

@@ -26,7 +26,7 @@ HALF_V = V // 2
 PIECE = 256
 SPARE = 865
 GROUP = 128
-SPLIT = 320
+SPLIT = 288
 PAIR = 2
 MX_ALIGN = 64
 

@@ -13,6 +13,7 @@ U16 = mybir.dt.uint16
 U8 = mybir.dt.uint8
 FP8X4 = mybir.dt.float8_e4m3fn_x4
 ADD = mybir.AluOpType.add
+COPY = mybir.ActivationFunctionType.Copy
 
 P = 128
 PACK = 4
@@ -24,7 +25,6 @@ LINE = 4
 HALF_S = S // 2
 HALF_V = V // 2
 PIECE = 256
-SPARE = 865
 GROUP = 128
 SPLIT = 288
 PAIR = 2
@@ -90,8 +90,7 @@ def tile_picked_fpn_none_p_kernel(
                 g_s[X_ROWS + ROWS * q : X_ROWS + ROWS * (q + 1), :].bitcast(I32),
             )
 
-        t_sb = sb.tile([P, V + SPARE], F32, name="t_sb")
-        nc.vector.memset(t_sb[:, V:], 0.0)
+        t_sb = sb.tile([P, V], F32, name="t_sb")
         s_bf = sb.tile([P, V, PACK], BF16, name="s_bf", align_bytes=MX_ALIGN)
 
         for rows, c0, c1 in (
@@ -100,7 +99,7 @@ def tile_picked_fpn_none_p_kernel(
             (slice(PAIR, PACK), GROUP, 2 * GROUP),
             (slice(PAIR, PACK), 2 * GROUP, SPLIT),
         ):
-            nc.scalar.copy(s_bf[:, c0:c1, rows], s_raw[:, rows, c0:c1].rearrange("p t c -> p c t"))
+            nc.scalar.activation(s_bf[:, c0:c1, rows], s_raw[:, rows, c0:c1].rearrange("p t c -> p c t"), COPY)
         for c0, c1 in ((V - GROUP, V), (SPLIT, V - GROUP)):
             nc.vector.tensor_copy(
                 s_bf[:, c0:c1, :].rearrange("p (c i) t -> p c t i", i=LINE),
@@ -128,7 +127,8 @@ def tile_picked_fpn_none_p_kernel(
             nc.scalar.copy(t_sb[:, v0 : v0 + width], t_ps[:])
 
         t_g = sb.tile([P, S], F32, name="t_g")
-        nc.vector.tensor_copy(t_g[:], t_sb[:].indirect(par_sb[:]))
+        for j0, count in ((0, 384), (384, 384), (768, 256)):
+            nc.scalar.activation(t_g[:, j0 : j0 + count], t_sb[:].indirect(entries(par_sb, j0, count)), COPY)
 
         g_w = [sb.tile([P, HALF_S], U32, name="g_w%d" % h, align_bytes=MX_ALIGN) for h in range(2)]
         for h in range(2):

@@ -26,6 +26,7 @@ HALF_S = S // 2
 HALF_V = V // 2
 PIECE = 256
 GROUP = 128
+GATHERS = ((0, 512), (512, 256), (768, 256))
 SPLIT = 288
 PAIR = 2
 MX_ALIGN = 64
@@ -130,14 +131,17 @@ def tile_picked_fpn_none_p_kernel(
         for j0, count in ((0, 384), (384, 384), (768, 256)):
             nc.scalar.activation(t_g[:, j0 : j0 + count], t_sb[:].indirect(entries(par_sb, j0, count)), COPY)
 
-        g_w = [sb.tile([P, HALF_S], U32, name="g_w%d" % h, align_bytes=MX_ALIGN) for h in range(2)]
-        for h in range(2):
-            nc.vector.tensor_copy(g_w[h][:], x_w[:].indirect(entries(offs_sb, h * HALF_S, HALF_S)))
+        g_w = {}
+        for first, count in GATHERS:
+            piece = sb.tile([P, count], U32, name="g_w%d" % first, align_bytes=MX_ALIGN)
+            nc.vector.tensor_copy(piece[:], x_w[:].indirect(entries(offs_sb, first, count)))
+            for j0 in range(first, first + count, GROUP):
+                g_w[j0] = (piece, j0 - first)
 
         stores = (
             (0, PIECE, 1, nc.sync),
             (PIECE, PIECE, 1, nc.scalar),
-            (HALF_S, GROUP, 2, nc.sync),
+            (HALF_S, PIECE, 1, nc.sync),
             (HALF_S + PIECE, GROUP, 1, nc.scalar),
             (S - GROUP, GROUP, 1, nc.sync),
         )
@@ -145,13 +149,13 @@ def tile_picked_fpn_none_p_kernel(
         for first, width, count, queue in stores:
             res = sb.tile([P, width * count], F32, name="res%d" % first)
             for j0 in range(first, first + width * count, width):
-                h, c0 = divmod(j0, HALF_S)
+                piece, c0 = g_w[j0]
                 y_ps = ps.tile([P, width], F32, name="y_ps", tag=banks.pop(0))
                 nc.tensor.matmul_mx(
                     out=y_ps[:],
                     lhsT=w1_w[:].bitcast(FP8X4),
                     lhsT_scale=w1_s[:],
-                    rhs=g_w[h][:, c0 : c0 + width].bitcast(FP8X4),
+                    rhs=piece[:, c0 : c0 + width].bitcast(FP8X4),
                     rhs_scale=y_s[:, j0 : j0 + width],
                     start=True,
                     stop=True,

@@ -23,12 +23,9 @@ X_ROWS = P - 16
 LANES = 16
 LINE = 4
 HALF_S = S // 2
-HALF_V = V // 2
 PIECE = 256
 GROUP = 128
 GATHERS = ((0, 512), (512, 256), (768, 256))
-SPLIT = 288
-PAIR = 2
 MX_ALIGN = 64
 
 
@@ -74,13 +71,12 @@ def tile_picked_fpn_none_p_kernel(
         nc.sync.dma_start(offs_sb[:], offs)
         nc.scalar.dma_start(x_s[X_ROWS:P, :].bitcast(I32), x_scales[0].bitcast(I32))
         nc.sync.dma_start(par_sb[:], par)
-        nc.sync.dma_start(s_raw[:, 0:PAIR, :], s_rows[:, 0:PAIR, :])
-        nc.sync.dma_start(s_raw[:, PAIR:PACK, :], s_rows[:, PAIR:PACK, :])
         nc.sync.dma_start(w2_w[:].bitcast(I32), words_as_int32(w2_words))
+        nc.sync.dma_start(s_raw[:], s_rows)
         load_scale_rows(nc.sync, w2_s, w2_scales, range(4))
+        load_scale_rows(nc.sync, w1_s, w1_scales, (0, 1))
         nc.sync.dma_start(x_w[:].bitcast(I32), words_as_int32(x_words))
         nc.sync.dma_start(w1_w[:].bitcast(I32), words_as_int32(w1_words))
-        load_scale_rows(nc.gpsimd, w1_s, w1_scales, (0, 1))
         load_scale_rows(nc.sync, w1_s, w1_scales, (2, 3))
 
         g_s = sb.tile([P, S], U8, name="g_s", align_bytes=MX_ALIGN)
@@ -94,20 +90,15 @@ def tile_picked_fpn_none_p_kernel(
         t_sb = sb.tile([P, V], F32, name="t_sb")
         s_bf = sb.tile([P, V, PACK], BF16, name="s_bf", align_bytes=MX_ALIGN)
 
-        for rows, c0, c1 in (
-            (slice(0, PAIR), 0, SPLIT),
-            (slice(PAIR, PACK), 0, GROUP),
-            (slice(PAIR, PACK), GROUP, 2 * GROUP),
-            (slice(PAIR, PACK), 2 * GROUP, SPLIT),
-        ):
-            nc.scalar.activation(s_bf[:, c0:c1, rows], s_raw[:, rows, c0:c1].rearrange("p t c -> p c t"), COPY)
-        for c0, c1 in ((V - GROUP, V), (SPLIT, V - GROUP)):
-            nc.vector.tensor_copy(
-                s_bf[:, c0:c1, :].rearrange("p (c i) t -> p c t i", i=LINE),
-                s_raw[:, :, c0:c1].rearrange("p t (c i) -> p c t i", i=LINE),
-            )
+        for c0 in range(0, V, GROUP):
+            dst = s_bf[:, c0 : c0 + GROUP, :].rearrange("p (c i) t -> p c t i", i=LINE)
+            src = s_raw[:, :, c0 : c0 + GROUP].rearrange("p t (c i) -> p c t i", i=LINE)
+            if c0 < V // 2:
+                nc.scalar.activation(dst, src, COPY)
+            else:
+                nc.vector.tensor_copy(dst, src)
         width = GROUP
-        for n, v0 in enumerate((V - GROUP, 0, GROUP, 2 * GROUP)):
+        for n, v0 in enumerate((0, 2 * GROUP, GROUP, 3 * GROUP)):
             s_w = sb.tile([P, width], U32, name="s_w%d" % n, align_bytes=MX_ALIGN)
             s_s = sb.tile([P, width], U8, name="s_s%d" % n, align_bytes=MX_ALIGN)
             t_ps = ps.tile([P, width], F32, name="t_ps%d" % n)

from contextlib import ExitStack

import concourse.mybir as mybir

K, T, S, V, N = 512, 4096, 1024, 512, 128
FLOPS = 2 * K * N * (S + V)

F32 = mybir.dt.float32
BF16 = mybir.dt.bfloat16
I32 = mybir.dt.int32
U32 = mybir.dt.uint32
U16 = mybir.dt.uint16
U8 = mybir.dt.uint8
FP8X4 = mybir.dt.float8_e4m3fn_x4
ADD = mybir.AluOpType.add
COPY = mybir.ActivationFunctionType.Copy

P = 128
PACK = 4
QUADRANT = 32
ROWS = 4
X_ROWS = P - 16
LANES = 16
LINE = 4
HALF_S = S // 2
PIECE = 256
GROUP = 128
GATHERS = ((0, 512), (512, 256), (768, 256))
MX_ALIGN = 64


def words_as_int32(words):
    return words[0].rearrange("p n t -> p (n t)").bitcast(I32)


def quadrant_rows(q):
    return slice(QUADRANT * q, QUADRANT * q + ROWS)


def load_scale_rows(queue, plane, scales, quadrants):
    for q in quadrants:
        queue.dma_start(plane[quadrant_rows(q), :].bitcast(I32), scales[0, ROWS * q : ROWS * (q + 1), :].bitcast(I32))


def entries(lst, start, count):
    return lst[:, start // LANES : (start + count) // LANES]


def tile_picked_fpn_none_p_kernel(
    tc, x_words, x_scales, sT, w1_words, w1_scales, w2_words, w2_scales, offs, par, out
):
    nc = tc.nc
    with ExitStack() as ctx:
        sb = ctx.enter_context(tc.tile_pool(name="sb", bufs=1))
        ps = ctx.enter_context(tc.psum_pool(name="ps", bufs=1))

        offs_sb = sb.tile([P, S // LANES], U16, name="offs_sb")
        par_sb = sb.tile([P, S // LANES], U16, name="par_sb")
        s_raw = sb.tile([P, PACK, V], F32, name="s_raw")
        x_w = sb.tile([P, T], U32, name="x_w", align_bytes=MX_ALIGN)
        x_s = sb.tile([P, T], U8, name="x_s", align_bytes=MX_ALIGN)
        y_s = sb.tile([P, S], U8, name="y_s", align_bytes=MX_ALIGN)
        w1_w = sb.tile([P, N], U32, name="w1_w", align_bytes=MX_ALIGN)
        w2_w = sb.tile([P, N], U32, name="w2_w", align_bytes=MX_ALIGN)
        w1_s = sb.tile([P, N], U8, name="w1_s", align_bytes=MX_ALIGN)
        w2_s = sb.tile([P, N], U8, name="w2_s", align_bytes=MX_ALIGN)

        nc.vector.memset(x_s[0:X_ROWS, :].bitcast(I32), 0)

        s_rows = sT.rearrange("(p j) v -> p j v", j=PACK)
        nc.sync.dma_start(offs_sb[:], offs)
        nc.scalar.dma_start(x_s[X_ROWS:P, :].bitcast(I32), x_scales[0].bitcast(I32))
        nc.sync.dma_start(par_sb[:], par)
        nc.sync.dma_start(w2_w[:].bitcast(I32), words_as_int32(w2_words))
        nc.sync.dma_start(s_raw[:], s_rows)
        load_scale_rows(nc.sync, w2_s, w2_scales, range(4))
        load_scale_rows(nc.sync, w1_s, w1_scales, (0, 1))
        nc.sync.dma_start(x_w[:].bitcast(I32), words_as_int32(x_words))
        nc.sync.dma_start(w1_w[:].bitcast(I32), words_as_int32(w1_words))
        load_scale_rows(nc.sync, w1_s, w1_scales, (2, 3))

        g_s = sb.tile([P, S], U8, name="g_s", align_bytes=MX_ALIGN)
        nc.vector.tensor_copy(g_s[:], x_s[:].indirect(offs_sb[:]))
        for q in range(4):
            nc.sync.dma_start(
                y_s[quadrant_rows(q), :].bitcast(I32),
                g_s[X_ROWS + ROWS * q : X_ROWS + ROWS * (q + 1), :].bitcast(I32),
            )

        t_sb = sb.tile([P, V], F32, name="t_sb")
        s_bf = sb.tile([P, V, PACK], BF16, name="s_bf", align_bytes=MX_ALIGN)

        for c0 in range(0, V, GROUP):
            dst = s_bf[:, c0 : c0 + GROUP, :].rearrange("p (c i) t -> p c t i", i=LINE)
            src = s_raw[:, :, c0 : c0 + GROUP].rearrange("p t (c i) -> p c t i", i=LINE)
            if c0 < V // 2:
                nc.scalar.activation(dst, src, COPY)
            else:
                nc.vector.tensor_copy(dst, src)
        width = GROUP
        for n, v0 in enumerate((0, 2 * GROUP, GROUP, 3 * GROUP)):
            s_w = sb.tile([P, width], U32, name="s_w%d" % n, align_bytes=MX_ALIGN)
            s_s = sb.tile([P, width], U8, name="s_s%d" % n, align_bytes=MX_ALIGN)
            t_ps = ps.tile([P, width], F32, name="t_ps%d" % n)
            nc.vector.quantize_mx(
                out=s_w[:].bitcast(FP8X4),
                scales=s_s[:],
                in_=s_bf[:, v0 : v0 + width, :].rearrange("p v t -> p (v t)"),
            )
            nc.tensor.matmul_mx(
                out=t_ps[:],
                lhsT=w2_w[:].bitcast(FP8X4),
                lhsT_scale=w2_s[:],
                rhs=s_w[:].bitcast(FP8X4),
                rhs_scale=s_s[:],
                start=True,
                stop=True,
            )
            nc.scalar.copy(t_sb[:, v0 : v0 + width], t_ps[:])

        t_g = sb.tile([P, S], F32, name="t_g")
        for j0, count in ((0, 384), (384, 384), (768, 256)):
            nc.scalar.activation(t_g[:, j0 : j0 + count], t_sb[:].indirect(entries(par_sb, j0, count)), COPY)

        g_w = {}
        for first, count in GATHERS:
            piece = sb.tile([P, count], U32, name="g_w%d" % first, align_bytes=MX_ALIGN)
            nc.vector.tensor_copy(piece[:], x_w[:].indirect(entries(offs_sb, first, count)))
            for j0 in range(first, first + count, GROUP):
                g_w[j0] = (piece, j0 - first)

        stores = (
            (0, PIECE, 1, nc.sync),
            (PIECE, PIECE, 1, nc.scalar),
            (HALF_S, PIECE, 1, nc.sync),
            (HALF_S + PIECE, GROUP, 1, nc.scalar),
            (S - GROUP, GROUP, 1, nc.sync),
        )
        banks = ["y_ps0", "y_ps1", "y_ps2", "y_ps3", "t_ps0", "t_ps1"]
        for first, width, count, queue in stores:
            res = sb.tile([P, width * count], F32, name="res%d" % first)
            for j0 in range(first, first + width * count, width):
                piece, c0 = g_w[j0]
                y_ps = ps.tile([P, width], F32, name="y_ps", tag=banks.pop(0))
                nc.tensor.matmul_mx(
                    out=y_ps[:],
                    lhsT=w1_w[:].bitcast(FP8X4),
                    lhsT_scale=w1_s[:],
                    rhs=piece[:, c0 : c0 + width].bitcast(FP8X4),
                    rhs_scale=y_s[:, j0 : j0 + width],
                    start=True,
                    stop=True,
                )
                nc.vector.tensor_tensor(res[:, j0 - first : j0 - first + width], y_ps[:], t_g[:, j0 : j0 + width], ADD)
            queue.dma_start(out[:, first : first + width * count], res[:])
